import numpy as np
import ml_dtypes


def mxq(x, axis, fmt="e4m3"):
    dtype, down = {"e4m3": (ml_dtypes.float8_e4m3fn, 7), "e5m2": (ml_dtypes.float8_e5m2, 14)}[fmt]
    v = np.moveaxis(np.asarray(x, np.float32).astype(ml_dtypes.bfloat16).astype(np.float64), axis, -1)
    blocks = v.reshape(v.shape[:-1] + (-1, 32))
    amax = np.abs(blocks).max(-1, keepdims=True)
    byte = np.maximum(np.where(amax > 0, np.frexp(amax)[1] - 1 + 127, 0) - down, 1)
    scale = np.exp2(byte - 127.0)
    codes = (blocks / scale).astype(np.float32).astype(dtype).astype(np.float64)
    return np.moveaxis((codes * scale).reshape(v.shape), -1, axis)


WIDE = False


def mx_kscale(k):
    if not WIDE:
        return np.ones(k)
    levels = np.array([10, -10, 5, -5, 0])
    if k % 512:
        return np.exp2(np.random.permutation(np.resize(levels, k // 32))).repeat(32)
    a = np.empty((k // 512, 16))
    for p in range(k // 512):
        a[p, :8] = np.random.permutation(np.resize(levels, 8))
        for g in range(8):
            far = levels[np.abs(levels - a[p, g]) >= 10]
            a[p, g + 8] = far[np.random.randint(len(far))]
    return np.exp2(a.ravel()).repeat(32)


def f64(x):
    return np.asarray(x).astype(np.float64)


def striped(idx):
    return np.tile(idx.reshape(-1, 16).T, (8, 1)).astype(np.uint16)


def unstriped(offs):
    return offs[:16].T.reshape(-1).astype(np.int64)


def striped8(idx):
    return np.concatenate([x.reshape(-1, 16).T for x in idx]).astype(np.uint16)


def runs(offs, k):
    lists = np.stack([offs[16 * r : 16 * r + 16].T.reshape(-1) for r in range(8)]).astype(np.int64)
    return lists[np.arange(k) % 512 // 64]


def pack_weight(w):
    k, n = w.shape
    w = f64(np.asarray(w, np.float32).astype(ml_dtypes.bfloat16)).reshape(k // 32, 32, n)
    amax = np.abs(w).max(1)
    byte = np.clip(np.where(amax > 0, np.frexp(amax)[1] - 1 + 127 - 7, 1), 1, 254)
    scaled = (w * np.exp2(127.0 - byte)[:, None, :]).reshape(k, n).astype(np.float32)
    words = np.ascontiguousarray(scaled.reshape(k // 512, 128, 4, n).transpose(0, 1, 3, 2)).astype(ml_dtypes.float8_e4m3fn).view(np.uint8)
    return words, np.ascontiguousarray(byte.astype(np.uint8).reshape(k // 512, 16, n))


def unpack_weight(words, scales):
    g, p, n, _ = words.shape
    vals = np.ascontiguousarray(words).view(ml_dtypes.float8_e4m3fn).astype(np.float64) * np.repeat(np.exp2(scales.astype(np.float64) - 127.0), 8, axis=1)[..., None]
    return vals.transpose(0, 1, 3, 2).reshape(g * 512, n)


E2M1 = np.array([0.0, 0.5, 1.0, 1.5, 2.0, 3.0, 4.0, 6.0, -0.0, -0.5, -1.0, -1.5, -2.0, -3.0, -4.0, -6.0])


def pack_fp4(w):
    k, n = w.shape
    w = f64(np.asarray(w, np.float32).astype(ml_dtypes.bfloat16)).reshape(k // 32, 32, n)
    amax = np.abs(w).max(1)
    mant, ex = np.frexp(amax / 6.0)
    byte = np.clip(np.where(amax > 0, np.where(mant > 0.5, ex, ex - 1) + 127, 1), 1, 254)
    scaled = (w * np.exp2(127.0 - byte)[:, None, :]).reshape(k, n).astype(np.float32)
    c = np.ascontiguousarray(scaled.reshape(k // 512, 128, 4, n).transpose(0, 1, 3, 2)).astype(ml_dtypes.float4_e2m1fn).view(np.uint8) & 0xF
    words = (c[..., 0::2] | (c[..., 1::2] << 4)).reshape(k // 512, 128, 2 * n)
    return np.ascontiguousarray(words), np.ascontiguousarray(byte.astype(np.uint8).reshape(k // 512, 16, n))


def unpack_fp4(words, scales):
    g, _, n = scales.shape
    words = np.ascontiguousarray(words).reshape(g, 128, n, 2)
    nib = np.empty((g, 128, n, 4), np.uint8)
    nib[..., 0::2] = words & 0xF
    nib[..., 1::2] = words >> 4
    vals = E2M1[nib] * np.repeat(np.exp2(scales.astype(np.float64) - 127.0), 8, axis=1)[..., None]
    return vals.transpose(0, 1, 3, 2).reshape(g * 512, n)


def sigmoid(v):
    return 1.0 / (1.0 + np.exp(-np.maximum(v, -700.0)))

def planes(y):
    n, m = y.shape
    v = y.astype(np.float32).astype(ml_dtypes.bfloat16).astype(np.float64).reshape(n // 32, 32, m)
    top = np.abs(v).max(1)
    byte = np.clip(np.where(top > 0, np.frexp(top)[1] - 1 + 127 - 7, 1), 1, 254)
    codes = (v * np.exp2(127.0 - byte)[:, None, :]).reshape(n, m).astype(np.float32).astype(ml_dtypes.float8_e4m3fn).view(np.uint8)
    words = codes.reshape(n // 512, 128, 4, m).transpose(0, 1, 3, 2)
    return np.ascontiguousarray(words), np.ascontiguousarray(byte.astype(np.uint8).reshape(n // 512, 16, m))


K, T, S, V, N, G, H = 512, 2048, 512, 256, 512, 2048, 512


def setup_inputs():
    n = np.random.standard_normal
    s = mx_kscale(K)[:, None]
    u = mx_kscale(S)
    packed_xT = pack_weight(n((K, T)) * s)
    packed_dT = pack_weight(n((K, G)) / s)
    packed_w1 = pack_fp4(n((H, N)) / np.sqrt(H) / u[:, None])
    return {
        "x_words": packed_xT[0],
        "x_scales": packed_xT[1],
        "d_words": packed_dT[0],
        "d_scales": packed_dT[1],
        "gn": (np.random.uniform(0.5, 1.5, (H, 1)) * u[:, None]).astype(np.float32),
        "w1_words": packed_w1[0],
        "w1_scales": packed_w1[1],
        "offs": striped8(np.random.randint(0, T, (8, S))),
        "k1": striped8(np.random.randint(0, G, (8, H))),
        "n1": striped(np.random.permutation(S)),
        "n2": striped(np.random.permutation(V)),
        "n3": striped(np.random.permutation(V)),
    }


def reference(x_words, x_scales, d_words, d_scales, gn, w1_words, w1_scales, offs, k1, n1, n2, n3):
    d_k1 = unpack_weight(d_words, d_scales)[np.arange(K)[:, None], runs(k1, K)]
    xq = unpack_weight(x_words, x_scales)[np.arange(K)[:, None], runs(offs, K)]
    h = 0.0625 * (d_k1.T @ xq)
    ln = h[:, unstriped(n1)]
    sq = (ln) ** 2
    ms = sq.reshape(H, V, 2).sum(axis=2)
    z = f64(gn) * np.sqrt(ms + 0.1)
    h2 = unpack_fp4(w1_words, w1_scales).T @ mxq(z, 0, "e4m3")
    out_0 = h2 + (sigmoid(h2[:, unstriped(n2)])) * (h2[:, unstriped(n3)] - h2)
    return (out_0,) + planes(out_0)

@@ -1,0 +1,228 @@
+from contextlib import ExitStack
+
+import concourse.mybir as mybir
+
+K, T, S, V, N, H = 512, 2048, 512, 256, 512, 512
+FLOPS = 2 * K * H * S + 2 * H * N * V
+
+F32 = mybir.dt.float32
+BF16 = mybir.dt.bfloat16
+I32 = mybir.dt.int32
+U32 = mybir.dt.uint32
+U16 = mybir.dt.uint16
+U8 = mybir.dt.uint8
+FP8X4 = mybir.dt.float8_e4m3fn_x4
+FP4X4 = mybir.dt.float4_e2m1fn_x4
+ACT = mybir.ActivationFunctionType
+ALU = mybir.AluOpType
+
+P = 128
+PACK = 4
+HALF_S = S // 2
+HALF_V = V // 2
+PER_COL = 16
+
+
+def tile_picked_hpqhprmstrack_none_po_kernel(
+    tc, x_words, x_scales, d_words, d_scales, gn, w1_words, w1_scales, offs, k1, n1, n2, n3, out_0, out_1, out_2
+):
+    nc = tc.nc
+    with ExitStack() as ctx:
+        sb = ctx.enter_context(tc.tile_pool(name="sb", bufs=1))
+        ps = ctx.enter_context(tc.psum_pool(name="ps", bufs=1))
+
+        def load_list(src, name):
+            tile = sb.tile(list(src.shape), U16, name=name)
+            nc.sync.dma_start(out=tile[:], in_=src)
+            return tile
+
+        def load_scale_table(src, name):
+            tile = sb.tile([P, T], U8, name=name, tag=name, align_bytes=64)
+            nc.vector.memset(tile[:].bitcast(I32), 0)
+            nc.scalar.dma_start(out=tile[0:P:8, :].bitcast(I32), in_=src[0].bitcast(I32))
+            return tile
+
+        def load_word_table(src, name):
+            tile = sb.tile([P, T], I32, name=name, tag=name, align_bytes=64)
+            nc.sync.dma_start(out=tile[:], in_=src[0].rearrange("p n t -> p (n t)").bitcast(I32))
+            return tile
+
+        k1_sb = load_list(k1, "k1_sb")
+        offs_sb = load_list(offs, "offs_sb")
+        d_scale_table = load_scale_table(d_scales, "d_scale_table")
+        x_scale_table = load_scale_table(x_scales, "x_scale_table")
+        d_word_table = load_word_table(d_words, "d_word_table")
+        n1_sb = load_list(n1, "n1_sb")
+        n2_sb = load_list(n2, "n2_sb")
+        n3_sb = load_list(n3, "n3_sb")
+        x_word_table = load_word_table(x_words, "x_word_table")
+
+        w1_scale_raw = sb.tile([P, N], U8, align_bytes=64)
+        nc.gpsimd.memset(w1_scale_raw[:].bitcast(I32), 0)
+        w1_raw = sb.tile([P, 2 * N], U8, align_bytes=64)
+        nc.gpsimd.dma_start(out=w1_raw[:].bitcast(I32), in_=w1_words[0].bitcast(I32))
+        for q in range(4):
+            nc.gpsimd.dma_start(
+                out=w1_scale_raw[32 * q : 32 * q + 4, :].bitcast(I32), in_=w1_scales[0, 4 * q : 4 * q + 4, :].bitcast(I32)
+            )
+        gain = sb.tile([P, PACK], F32)
+        nc.gpsimd.dma_start(out=gain[:], in_=gn.rearrange("(p t) o -> p (t o)", t=PACK))
+
+        d_scale_picked = sb.tile([P, H], U8, align_bytes=64)
+        nc.vector.tensor_copy(out=d_scale_picked[:], in_=d_scale_table[:].indirect(k1_sb[:]))
+        planes = sb.tile([P, H + S], U8, align_bytes=64)
+        nc.vector.tensor_copy(
+            out=planes[:, 0:H].rearrange("p (t m) -> p m t", t=PACK),
+            in_=d_scale_picked[:].rearrange("p (m t) -> p m t", t=PACK),
+        )
+        x_scale_picked = sb.tile([P, S], U8, align_bytes=64)
+        nc.vector.tensor_copy(out=x_scale_picked[:], in_=x_scale_table[:].indirect(offs_sb[:]))
+        nc.vector.tensor_copy(out=planes[:, H : H + S].bitcast(I32), in_=x_scale_picked[:].bitcast(I32))
+        for s in range(1, 4):
+            nc.scalar.dma_start(out=planes[s:P:32, :].bitcast(I32), in_=planes[8 * s : P : 32, :].bitcast(I32))
+
+        w1_dealt = sb.tile([P, 2 * N], U8, align_bytes=64)
+        nc.scalar.copy(
+            out=w1_dealt[:].bitcast(U16).rearrange("p (t m) -> p m t", t=PACK),
+            in_=w1_raw[:].bitcast(U16).rearrange("p (m t) -> p m t", t=PACK),
+        )
+
+        d_picked = sb.tile([P, H], U32, tag="x_scale_table", align_bytes=64)
+        nc.vector.tensor_copy(out=d_picked[:], in_=d_word_table[:].bitcast(U32).indirect(k1_sb[:]))
+        d_dealt = sb.tile([P, H], U32, align_bytes=64)
+        nc.vector.tensor_copy(
+            out=d_dealt[:].rearrange("p (t m) -> p m t", t=PACK), in_=d_picked[:].rearrange("p (m t) -> p m t", t=PACK)
+        )
+        x_picked = []
+        for c in range(2):
+            tile = sb.tile([P, HALF_S], U32, name="x_picked%d" % c, tag=("d_word_table", "x_scale_table")[c], align_bytes=64)
+            cols = slice(c * HALF_S // PER_COL, (c + 1) * HALF_S // PER_COL)
+            nc.vector.tensor_copy(out=tile[:], in_=x_word_table[:].bitcast(U32).indirect(offs_sb[:, cols]))
+            x_picked.append(tile)
+        w1_scale_dealt = sb.tile([P, N], U8, align_bytes=64)
+        nc.vector.tensor_copy(
+            out=w1_scale_dealt[:].rearrange("p (t m) -> p m t", t=PACK),
+            in_=w1_scale_raw[:].rearrange("p (m t) -> p m t", t=PACK),
+        )
+
+        squares = [sb.tile([P, S], F32, name="squares%d" % t) for t in range(PACK)]
+        for t, c in ((0, 0), (1, 0), (0, 1), (1, 1), (2, 0), (2, 1), (3, 0), (3, 1)):
+            bank = ps.tile([P, HALF_S], F32, name="h_bank", tag="bank%d" % (2 * t + c))
+            nc.tensor.matmul_mx(
+                out=bank[:],
+                lhsT=d_dealt[:, t * P : (t + 1) * P].bitcast(FP8X4),
+                lhsT_scale=planes[:, t * P : (t + 1) * P],
+                rhs=x_picked[c][:].bitcast(FP8X4),
+                rhs_scale=planes[:, H + c * HALF_S : H + (c + 1) * HALF_S],
+                start=True,
+                stop=True,
+            )
+            nc.scalar.activation(
+                out=squares[t][:, c * HALF_S : (c + 1) * HALF_S], in_=bank[:], func=ACT.Square, scale=0.0625
+            )
+
+        lined = [sb.tile([P, PACK, HALF_S], F32, name="lined%d" % c) for c in range(2)]
+
+        def line_up(t, c, on_scalar):
+            window = squares[t][:].indirect(n1_sb[:, c * HALF_S // PER_COL : (c + 1) * HALF_S // PER_COL])
+            if on_scalar:
+                nc.scalar.activation(out=lined[c][:, t, :], in_=window, func=ACT.Copy)
+            else:
+                nc.vector.tensor_copy(out=lined[c][:, t, :], in_=window)
+
+        for t in range(PACK):
+            line_up(t, 0, False)
+        for t in range(PACK):
+            line_up(t, 1, t != 2)
+
+        h2_rows = [sb.tile([P, V], F32, name="h2_rows%d" % t) for t in range(PACK)]
+        h2_banks = []
+        sums, roots = [], []
+        for c in range(2):
+            pair_sums = sb.tile([P, PACK, HALF_V], F32, name="pair_sums%d" % c)
+            pairs = lined[c][:].rearrange("p t (v e) -> p (t v) e", e=2)
+            nc.vector.tensor_tensor(
+                out=pair_sums[:].rearrange("p t v -> p (t v)"), in0=pairs[:, :, 0], in1=pairs[:, :, 1], op=ALU.add
+            )
+            sums.append(pair_sums)
+        for c in range(2):
+            root = sb.tile([P, HALF_V, PACK], F32, name="root%d" % c)
+            nc.scalar.activation(out=root[:], in_=sums[c][:].rearrange("p t v -> p v t"), func=ACT.Sqrt, bias=0.1)
+            roots.append(root)
+        for c in range(2):
+            z = sb.tile([P, HALF_V, PACK], BF16, name="z%d" % c, align_bytes=64)
+            nc.vector.tensor_tensor(
+                out=z[:], in0=roots[c][:], in1=gain[:].unsqueeze(1).to_broadcast([P, HALF_V, PACK]), op=ALU.mult
+            )
+            z_codes = sb.tile([P, HALF_V], U32, name="z_codes%d" % c, align_bytes=64)
+            z_scales = sb.tile([P, HALF_V], U8, name="z_scales%d" % c, align_bytes=64)
+            nc.vector.quantize_mx(
+                out=z_codes[:].bitcast(FP8X4), scales=z_scales[:], in_=z[:].rearrange("p v t -> p (v t)")
+            )
+            bank = ps.tile([P, PACK, HALF_V], F32, name="h2_bank", tag="bank%d" % c)
+            for t in range(PACK):
+                nc.tensor.matmul_mx(
+                    out=bank[:, t, :],
+                    lhsT=w1_dealt[:, 2 * t * P : 2 * (t + 1) * P].bitcast(FP4X4),
+                    lhsT_scale=w1_scale_dealt[:, t * P : (t + 1) * P],
+                    rhs=z_codes[:].bitcast(FP8X4),
+                    rhs_scale=z_scales[:],
+                    start=True,
+                    stop=True,
+                )
+            h2_banks.append(bank)
+        for c in range(2):
+            for t in range(PACK):
+                nc.vector.tensor_copy(out=h2_rows[t][:, c * HALF_V : (c + 1) * HALF_V], in_=h2_banks[c][:, t, :])
+
+        def half_of(lst, c):
+            return lst[:, c * HALF_V // PER_COL : (c + 1) * HALF_V // PER_COL]
+
+        gates = [sb.tile([P, PACK, HALF_V], F32, name="gates%d" % c) for c in range(2)]
+        other = [sb.tile([P, PACK, HALF_V], F32, name="other%d" % c) for c in range(2)]
+        mid = [sb.tile([P, PACK, HALF_V], F32, name="mid%d" % c) for c in range(2)]
+        result = [sb.tile([P, PACK, HALF_V], F32, name="result%d" % c) for c in range(2)]
+        for t in range(PACK):
+            nc.scalar.activation(out=gates[0][:, t, :], in_=h2_rows[t][:].indirect(half_of(n2_sb, 0)), func=ACT.Sigmoid)
+        for t in range(PACK):
+            nc.scalar.activation(out=other[1][:, t, :], in_=h2_rows[t][:].indirect(half_of(n3_sb, 1)), func=ACT.Copy)
+        for t in range(PACK):
+            nc.scalar.activation(out=gates[1][:, t, :], in_=h2_rows[t][:].indirect(half_of(n2_sb, 1)), func=ACT.Sigmoid)
+
+        def flat(tile):
+            return tile[:].rearrange("p t v -> p (t v)")
+
+        for t in range(PACK):
+            nc.vector.tensor_tensor(
+                out=other[0][:, t, :], in0=h2_rows[t][:].indirect(half_of(n3_sb, 0)), in1=gates[0][:, t, :], op=ALU.mult
+            )
+        nc.vector.scalar_tensor_tensor(
+            out=flat(mid[0]), in0=flat(gates[0]), scalar=1.0, in1=flat(h2_banks[0]), op0=ALU.subtract, op1=ALU.mult
+        )
+        nc.vector.tensor_tensor(out=flat(result[0]), in0=flat(other[0]), in1=flat(mid[0]), op=ALU.subtract)
+        diff = sb.tile([P, PACK, HALF_V], F32)
+        nc.vector.tensor_tensor(out=flat(diff), in0=flat(other[1]), in1=flat(h2_banks[1]), op=ALU.subtract)
+        nc.vector.tensor_tensor(out=flat(mid[1]), in0=flat(diff), in1=flat(gates[1]), op=ALU.mult)
+        nc.vector.tensor_tensor(out=flat(result[1]), in0=flat(mid[1]), in1=flat(h2_banks[1]), op=ALU.add)
+
+        out_rows = out_0.rearrange("(p t) v -> p t v", t=PACK)
+        out_words = out_1[0].rearrange("p v t -> p (v t)").bitcast(I32)
+        out_scales = sb.tile([P, V], U8, align_bytes=64)
+        for c in range(2):
+            cols = slice(c * HALF_V, (c + 1) * HALF_V)
+            nc.sync.dma_start(out=out_rows[:, :, cols], in_=result[c][:])
+            out_bf = sb.tile([P, HALF_V, PACK], BF16, name="out_bf%d" % c, align_bytes=64)
+            if c == 0:
+                nc.scalar.copy(out=out_bf[:], in_=result[c][:].rearrange("p t v -> p v t"))
+            else:
+                nc.vector.tensor_copy(out=out_bf[:], in_=result[c][:].rearrange("p t v -> p v t"))
+            out_codes = sb.tile([P, HALF_V], I32, name="out_codes%d" % c, align_bytes=64)
+            nc.vector.quantize_mx(
+                out=out_codes[:].bitcast(FP8X4), scales=out_scales[:, cols], in_=out_bf[:].rearrange("p v t -> p (v t)")
+            )
+            nc.sync.dma_start(out=out_words[:, cols], in_=out_codes[:])
+        for q in range(4):
+            queue = nc.scalar if q % 2 == 0 else nc.sync
+            queue.dma_start(
+                out=out_2[0, 4 * q : 4 * q + 4, :].bitcast(I32), in_=out_scales[32 * q : 32 * q + 4, :].bitcast(I32)
+            )

@@ -38,8 +38,8 @@ def tile_picked_hpqhprmstrack_none_po_kernel(
 
         def load_scale_table(src, name):
             tile = sb.tile([P, T], U8, name=name, tag=name, align_bytes=64)
-            nc.vector.memset(tile[:].bitcast(I32), 0)
-            nc.scalar.dma_start(out=tile[0:P:8, :].bitcast(I32), in_=src[0].bitcast(I32))
+            rows = src[0].bitcast(I32).unsqueeze(1).to_broadcast([16, 8, T // 4])
+            nc.sync.dma_start(out=tile[:].bitcast(I32), in_=rows)
             return tile
 
         def load_word_table(src, name):
@@ -48,25 +48,25 @@ def tile_picked_hpqhprmstrack_none_po_kernel(
             return tile
 
         k1_sb = load_list(k1, "k1_sb")
-        offs_sb = load_list(offs, "offs_sb")
         d_scale_table = load_scale_table(d_scales, "d_scale_table")
+        offs_sb = load_list(offs, "offs_sb")
         x_scale_table = load_scale_table(x_scales, "x_scale_table")
         d_word_table = load_word_table(d_words, "d_word_table")
         n1_sb = load_list(n1, "n1_sb")
         n2_sb = load_list(n2, "n2_sb")
         n3_sb = load_list(n3, "n3_sb")
         x_word_table = load_word_table(x_words, "x_word_table")
+        w1_raw = sb.tile([P, 2 * N], U8, align_bytes=64)
+        nc.sync.dma_start(out=w1_raw[:].bitcast(I32), in_=w1_words[0].bitcast(I32))
+        gain = sb.tile([P, PACK], F32)
+        nc.sync.dma_start(out=gain[:], in_=gn.rearrange("(p t) o -> p (t o)", t=PACK))
 
         w1_scale_raw = sb.tile([P, N], U8, align_bytes=64)
         nc.gpsimd.memset(w1_scale_raw[:].bitcast(I32), 0)
-        w1_raw = sb.tile([P, 2 * N], U8, align_bytes=64)
-        nc.gpsimd.dma_start(out=w1_raw[:].bitcast(I32), in_=w1_words[0].bitcast(I32))
         for q in range(4):
             nc.gpsimd.dma_start(
                 out=w1_scale_raw[32 * q : 32 * q + 4, :].bitcast(I32), in_=w1_scales[0, 4 * q : 4 * q + 4, :].bitcast(I32)
             )
-        gain = sb.tile([P, PACK], F32)
-        nc.gpsimd.dma_start(out=gain[:], in_=gn.rearrange("(p t) o -> p (t o)", t=PACK))
 
         d_scale_picked = sb.tile([P, H], U8, align_bytes=64)
         nc.vector.tensor_copy(out=d_scale_picked[:], in_=d_scale_table[:].indirect(k1_sb[:]))
@@ -75,13 +75,13 @@ def tile_picked_hpqhprmstrack_none_po_kernel(
             out=planes[:, 0:H].rearrange("p (t m) -> p m t", t=PACK),
             in_=d_scale_picked[:].rearrange("p (m t) -> p m t", t=PACK),
         )
-        x_scale_picked = sb.tile([P, S], U8, align_bytes=64)
+        x_scale_picked = sb.tile([P, S], U8, tag="x_scale_picked", align_bytes=64)
         nc.vector.tensor_copy(out=x_scale_picked[:], in_=x_scale_table[:].indirect(offs_sb[:]))
         nc.vector.tensor_copy(out=planes[:, H : H + S].bitcast(I32), in_=x_scale_picked[:].bitcast(I32))
         for s in range(1, 4):
             nc.scalar.dma_start(out=planes[s:P:32, :].bitcast(I32), in_=planes[8 * s : P : 32, :].bitcast(I32))
 
-        w1_dealt = sb.tile([P, 2 * N], U8, align_bytes=64)
+        w1_dealt = sb.tile([P, 2 * N], U8, tag="x_scale_picked", align_bytes=64)
         nc.scalar.copy(
             out=w1_dealt[:].bitcast(U16).rearrange("p (t m) -> p m t", t=PACK),
             in_=w1_raw[:].bitcast(U16).rearrange("p (m t) -> p m t", t=PACK),
@@ -99,7 +99,7 @@ def tile_picked_hpqhprmstrack_none_po_kernel(
             cols = slice(c * HALF_S // PER_COL, (c + 1) * HALF_S // PER_COL)
             nc.vector.tensor_copy(out=tile[:], in_=x_word_table[:].bitcast(U32).indirect(offs_sb[:, cols]))
             x_picked.append(tile)
-        w1_scale_dealt = sb.tile([P, N], U8, align_bytes=64)
+        w1_scale_dealt = sb.tile([P, N], U8, tag="x_word_table", align_bytes=64)
         nc.vector.tensor_copy(
             out=w1_scale_dealt[:].rearrange("p (t m) -> p m t", t=PACK),
             in_=w1_scale_raw[:].rearrange("p (m t) -> p m t", t=PACK),
@@ -136,7 +136,7 @@ def tile_picked_hpqhprmstrack_none_po_kernel(
             line_up(t, 1, t != 2)
 
         h2_rows = [sb.tile([P, V], F32, name="h2_rows%d" % t) for t in range(PACK)]
-        h2_banks = []
+        h2_banks, z_mx = [], []
         sums, roots = [], []
         for c in range(2):
             pair_sums = sb.tile([P, PACK, HALF_V], F32, name="pair_sums%d" % c)
@@ -159,21 +159,24 @@ def tile_picked_hpqhprmstrack_none_po_kernel(
             nc.vector.quantize_mx(
                 out=z_codes[:].bitcast(FP8X4), scales=z_scales[:], in_=z[:].rearrange("p v t -> p (v t)")
             )
-            bank = ps.tile([P, PACK, HALF_V], F32, name="h2_bank", tag="bank%d" % c)
-            for t in range(PACK):
-                nc.tensor.matmul_mx(
-                    out=bank[:, t, :],
-                    lhsT=w1_dealt[:, 2 * t * P : 2 * (t + 1) * P].bitcast(FP4X4),
-                    lhsT_scale=w1_scale_dealt[:, t * P : (t + 1) * P],
-                    rhs=z_codes[:].bitcast(FP8X4),
-                    rhs_scale=z_scales[:],
-                    start=True,
-                    stop=True,
-                )
+            z_mx.append((z_codes, z_scales))
+        for u in range(2):
+            bank = ps.tile([P, 2, V], F32, name="h2_bank", tag="bank%d" % u)
+            for c in range(2):
+                for e in range(2):
+                    t = 2 * u + e
+                    nc.tensor.matmul_mx(
+                        out=bank[:, e, c * HALF_V : (c + 1) * HALF_V],
+                        lhsT=w1_dealt[:, 2 * t * P : 2 * (t + 1) * P].bitcast(FP4X4),
+                        lhsT_scale=w1_scale_dealt[:, t * P : (t + 1) * P],
+                        rhs=z_mx[c][0][:].bitcast(FP8X4),
+                        rhs_scale=z_mx[c][1][:],
+                        start=True,
+                        stop=True,
+                    )
+            for e in range(2):
+                nc.vector.tensor_copy(out=h2_rows[2 * u + e][:], in_=bank[:, e, :])
             h2_banks.append(bank)
-        for c in range(2):
-            for t in range(PACK):
-                nc.vector.tensor_copy(out=h2_rows[t][:, c * HALF_V : (c + 1) * HALF_V], in_=h2_banks[c][:, t, :])
 
         def half_of(lst, c):
             return lst[:, c * HALF_V // PER_COL : (c + 1) * HALF_V // PER_COL]
@@ -184,26 +187,42 @@ def tile_picked_hpqhprmstrack_none_po_kernel(
         result = [sb.tile([P, PACK, HALF_V], F32, name="result%d" % c) for c in range(2)]
         for t in range(PACK):
             nc.scalar.activation(out=gates[0][:, t, :], in_=h2_rows[t][:].indirect(half_of(n2_sb, 0)), func=ACT.Sigmoid)
-        for t in range(PACK):
-            nc.scalar.activation(out=other[1][:, t, :], in_=h2_rows[t][:].indirect(half_of(n3_sb, 1)), func=ACT.Copy)
-        for t in range(PACK):
-            nc.scalar.activation(out=gates[1][:, t, :], in_=h2_rows[t][:].indirect(half_of(n2_sb, 1)), func=ACT.Sigmoid)
+        for u in range(2):
+            for t in (2 * u, 2 * u + 1):
+                nc.scalar.activation(out=other[1][:, t, :], in_=h2_rows[t][:].indirect(half_of(n3_sb, 1)), func=ACT.Copy)
+            for t in (2 * u, 2 * u + 1):
+                nc.scalar.activation(
+                    out=gates[1][:, t, :], in_=h2_rows[t][:].indirect(half_of(n2_sb, 1)), func=ACT.Sigmoid
+                )
+
+        def pair(tile, u):
+            return tile[:, 2 * u : 2 * u + 2, :]
 
         def flat(tile):
             return tile[:].rearrange("p t v -> p (t v)")
 
-        for t in range(PACK):
-            nc.vector.tensor_tensor(
-                out=other[0][:, t, :], in0=h2_rows[t][:].indirect(half_of(n3_sb, 0)), in1=gates[0][:, t, :], op=ALU.mult
+        for u in range(2):
+            for t in (2 * u, 2 * u + 1):
+                nc.vector.tensor_tensor(
+                    out=other[0][:, t, :],
+                    in0=h2_rows[t][:].indirect(half_of(n3_sb, 0)),
+                    in1=gates[0][:, t, :],
+                    op=ALU.mult,
+                )
+            nc.vector.scalar_tensor_tensor(
+                out=pair(mid[0], u),
+                in0=pair(gates[0], u),
+                scalar=1.0,
+                in1=h2_banks[u][:, :, 0:HALF_V],
+                op0=ALU.subtract,
+                op1=ALU.mult,
             )
-        nc.vector.scalar_tensor_tensor(
-            out=flat(mid[0]), in0=flat(gates[0]), scalar=1.0, in1=flat(h2_banks[0]), op0=ALU.subtract, op1=ALU.mult
-        )
         nc.vector.tensor_tensor(out=flat(result[0]), in0=flat(other[0]), in1=flat(mid[0]), op=ALU.subtract)
         diff = sb.tile([P, PACK, HALF_V], F32)
-        nc.vector.tensor_tensor(out=flat(diff), in0=flat(other[1]), in1=flat(h2_banks[1]), op=ALU.subtract)
-        nc.vector.tensor_tensor(out=flat(mid[1]), in0=flat(diff), in1=flat(gates[1]), op=ALU.mult)
-        nc.vector.tensor_tensor(out=flat(result[1]), in0=flat(mid[1]), in1=flat(h2_banks[1]), op=ALU.add)
+        for u in range(2):
+            nc.vector.tensor_tensor(out=pair(diff, u), in0=pair(other[1], u), in1=h2_banks[u][:, :, HALF_V:V], op=ALU.subtract)
+            nc.vector.tensor_tensor(out=pair(mid[1], u), in0=pair(diff, u), in1=pair(gates[1], u), op=ALU.mult)
+            nc.vector.tensor_tensor(out=pair(result[1], u), in0=pair(mid[1], u), in1=h2_banks[u][:, :, HALF_V:V], op=ALU.add)
 
         out_rows = out_0.rearrange("(p t) v -> p t v", t=PACK)
         out_words = out_1[0].rearrange("p v t -> p (v t)").bitcast(I32)

@@ -37,8 +37,9 @@ def tile_picked_hpqhprmstrack_none_po_kernel(
             return tile
 
         def load_scale_table(src, name):
-            tile = sb.tile([P, T], U8, name=name, tag=name, align_bytes=64)
-            rows = src[0].bitcast(I32).unsqueeze(1).to_broadcast([16, 8, T // 4])
+            width = src.shape[2]
+            tile = sb.tile([P, width], U8, name=name, tag=name, align_bytes=64)
+            rows = src[0].bitcast(I32).unsqueeze(1).to_broadcast([16, 8, width // 4])
             nc.sync.dma_start(out=tile[:].bitcast(I32), in_=rows)
             return tile
 
@@ -61,19 +62,21 @@ def tile_picked_hpqhprmstrack_none_po_kernel(
         gain = sb.tile([P, PACK], F32)
         nc.sync.dma_start(out=gain[:], in_=gn.rearrange("(p t) o -> p (t o)", t=PACK))
 
-        w1_scale_raw = sb.tile([P, N], U8, align_bytes=64)
-        nc.gpsimd.memset(w1_scale_raw[:].bitcast(I32), 0)
-        for q in range(4):
-            nc.gpsimd.dma_start(
-                out=w1_scale_raw[32 * q : 32 * q + 4, :].bitcast(I32), in_=w1_scales[0, 4 * q : 4 * q + 4, :].bitcast(I32)
-            )
+        w1_scale_raw = load_scale_table(w1_scales, "w1_scale_raw")
+
+        def dealt_view(ap, run):
+            return ap.rearrange("p (t a i) -> p a t i", t=PACK, i=run)
+
+        def plain_view(ap, run):
+            return ap.rearrange("p (a i t) -> p a t i", t=PACK, i=run)
+
 
         d_scale_picked = sb.tile([P, H], U8, align_bytes=64)
         nc.vector.tensor_copy(out=d_scale_picked[:], in_=d_scale_table[:].indirect(k1_sb[:]))
         planes = sb.tile([P, H + S], U8, align_bytes=64)
         nc.vector.tensor_copy(
-            out=planes[:, 0:H].rearrange("p (t m) -> p m t", t=PACK),
-            in_=d_scale_picked[:].rearrange("p (m t) -> p m t", t=PACK),
+            out=dealt_view(planes[:, 0:H], 16),
+            in_=plain_view(d_scale_picked[:], 16),
         )
         x_scale_picked = sb.tile([P, S], U8, tag="x_scale_picked", align_bytes=64)
         nc.vector.tensor_copy(out=x_scale_picked[:], in_=x_scale_table[:].indirect(offs_sb[:]))
@@ -83,15 +86,15 @@ def tile_picked_hpqhprmstrack_none_po_kernel(
 
         w1_dealt = sb.tile([P, 2 * N], U8, tag="x_scale_picked", align_bytes=64)
         nc.scalar.copy(
-            out=w1_dealt[:].bitcast(U16).rearrange("p (t m) -> p m t", t=PACK),
-            in_=w1_raw[:].bitcast(U16).rearrange("p (m t) -> p m t", t=PACK),
+            out=dealt_view(w1_dealt[:].bitcast(U16), 8),
+            in_=plain_view(w1_raw[:].bitcast(U16), 8),
         )
 
         d_picked = sb.tile([P, H], U32, tag="x_scale_table", align_bytes=64)
         nc.vector.tensor_copy(out=d_picked[:], in_=d_word_table[:].bitcast(U32).indirect(k1_sb[:]))
         d_dealt = sb.tile([P, H], U32, align_bytes=64)
         nc.vector.tensor_copy(
-            out=d_dealt[:].rearrange("p (t m) -> p m t", t=PACK), in_=d_picked[:].rearrange("p (m t) -> p m t", t=PACK)
+            out=dealt_view(d_dealt[:], 4), in_=plain_view(d_picked[:], 4)
         )
         x_picked = []
         for c in range(2):
@@ -101,9 +104,13 @@ def tile_picked_hpqhprmstrack_none_po_kernel(
             x_picked.append(tile)
         w1_scale_dealt = sb.tile([P, N], U8, tag="x_word_table", align_bytes=64)
         nc.vector.tensor_copy(
-            out=w1_scale_dealt[:].rearrange("p (t m) -> p m t", t=PACK),
-            in_=w1_scale_raw[:].rearrange("p (m t) -> p m t", t=PACK),
+            out=dealt_view(w1_scale_dealt[:], 16),
+            in_=plain_view(w1_scale_raw[:], 16),
         )
+        for s in range(1, 4):
+            nc.sync.dma_start(
+                out=w1_scale_dealt[s:P:32, :].bitcast(I32), in_=w1_scale_dealt[8 * s : P : 32, :].bitcast(I32)
+            )
 
         squares = [sb.tile([P, S], F32, name="squares%d" % t) for t in range(PACK)]
         for t, c in ((0, 0), (1, 0), (0, 1), (1, 1), (2, 0), (2, 1), (3, 0), (3, 1)):
@@ -229,12 +236,18 @@ def tile_picked_hpqhprmstrack_none_po_kernel(
         out_scales = sb.tile([P, V], U8, align_bytes=64)
         for c in range(2):
             cols = slice(c * HALF_V, (c + 1) * HALF_V)
-            nc.sync.dma_start(out=out_rows[:, :, cols], in_=result[c][:])
-            out_bf = sb.tile([P, HALF_V, PACK], BF16, name="out_bf%d" % c, align_bytes=64)
             if c == 0:
-                nc.scalar.copy(out=out_bf[:], in_=result[c][:].rearrange("p t v -> p v t"))
+                nc.sync.dma_start(out=out_rows[:, :, cols], in_=result[c][:])
             else:
-                nc.vector.tensor_copy(out=out_bf[:], in_=result[c][:].rearrange("p t v -> p v t"))
+                for u in range(2):
+                    nc.sync.dma_start(out=out_rows[:, 2 * u : 2 * u + 2, cols], in_=pair(result[c], u))
+            out_bf = sb.tile([P, HALF_V, PACK], BF16, name="out_bf%d" % c, align_bytes=64)
+            woven = out_bf[:].rearrange("p (a i) t -> p a t i", i=4)
+            runs = result[c][:].rearrange("p t (a i) -> p a t i", i=4)
+            if c == 0:
+                nc.scalar.copy(out=woven, in_=runs)
+            else:
+                nc.vector.tensor_copy(out=woven, in_=runs)
             out_codes = sb.tile([P, HALF_V], I32, name="out_codes%d" % c, align_bytes=64)
             nc.vector.quantize_mx(
                 out=out_codes[:].bitcast(FP8X4), scales=out_scales[:, cols], in_=out_bf[:].rearrange("p v t -> p (v t)")

@@ -18,9 +18,13 @@ ALU = mybir.AluOpType
 
 P = 128
 PACK = 4
+QUADRANT = 32
+BLOCK_PARTS = 8
+SCALE_ROWS = P // BLOCK_PARTS
+PER_COL = 16
+LINE = 16
 HALF_S = S // 2
 HALF_V = V // 2
-PER_COL = 16
 
 
 def tile_picked_hpqhprmstrack_none_po_kernel(
@@ -36,10 +40,10 @@ def tile_picked_hpqhprmstrack_none_po_kernel(
             nc.sync.dma_start(out=tile[:], in_=src)
             return tile
 
-        def load_scale_table(src, name):
+        def load_scale_rows(src, name):
             width = src.shape[2]
             tile = sb.tile([P, width], U8, name=name, tag=name, align_bytes=64)
-            rows = src[0].bitcast(I32).unsqueeze(1).to_broadcast([16, 8, width // 4])
+            rows = src[0].bitcast(I32).unsqueeze(1).to_broadcast([SCALE_ROWS, BLOCK_PARTS, width // 4])
             nc.sync.dma_start(out=tile[:].bitcast(I32), in_=rows)
             return tile
 
@@ -48,72 +52,72 @@ def tile_picked_hpqhprmstrack_none_po_kernel(
             nc.sync.dma_start(out=tile[:], in_=src[0].rearrange("p n t -> p (n t)").bitcast(I32))
             return tile
 
+        def deal(copy, dst, src, elem_bytes):
+            run = LINE // elem_bytes
+            copy(
+                out=dst.rearrange("p (t a i) -> p a t i", t=PACK, i=run),
+                in_=src.rearrange("p (a i t) -> p a t i", t=PACK, i=run),
+            )
+
+        def rows_to_plane(queue, tile):
+            for s in range(1, PACK):
+                queue.dma_start(
+                    out=tile[s:P:QUADRANT, :].bitcast(I32), in_=tile[BLOCK_PARTS * s : P : QUADRANT, :].bitcast(I32)
+                )
+
+        def entries(list_tile, c, count):
+            return list_tile[:, c * count // PER_COL : (c + 1) * count // PER_COL]
+
+        def couple(tile, u):
+            return tile[:, 2 * u : 2 * u + 2, :]
+
+        def flat(tile):
+            return tile[:].rearrange("p t v -> p (t v)")
+
+        d_scale_table = load_scale_rows(d_scales, "d_scale_table")
         k1_sb = load_list(k1, "k1_sb")
-        d_scale_table = load_scale_table(d_scales, "d_scale_table")
+        x_scale_table = load_scale_rows(x_scales, "x_scale_table")
         offs_sb = load_list(offs, "offs_sb")
-        x_scale_table = load_scale_table(x_scales, "x_scale_table")
         d_word_table = load_word_table(d_words, "d_word_table")
         n1_sb = load_list(n1, "n1_sb")
         n2_sb = load_list(n2, "n2_sb")
-        n3_sb = load_list(n3, "n3_sb")
         x_word_table = load_word_table(x_words, "x_word_table")
+        n3_sb = load_list(n3, "n3_sb")
         w1_raw = sb.tile([P, 2 * N], U8, align_bytes=64)
         nc.sync.dma_start(out=w1_raw[:].bitcast(I32), in_=w1_words[0].bitcast(I32))
         gain = sb.tile([P, PACK], F32)
         nc.sync.dma_start(out=gain[:], in_=gn.rearrange("(p t) o -> p (t o)", t=PACK))
-
-        w1_scale_raw = load_scale_table(w1_scales, "w1_scale_raw")
-
-        def dealt_view(ap, run):
-            return ap.rearrange("p (t a i) -> p a t i", t=PACK, i=run)
-
-        def plain_view(ap, run):
-            return ap.rearrange("p (a i t) -> p a t i", t=PACK, i=run)
-
+        w1_scale_raw = load_scale_rows(w1_scales, "w1_scale_raw")
 
         d_scale_picked = sb.tile([P, H], U8, align_bytes=64)
         nc.vector.tensor_copy(out=d_scale_picked[:], in_=d_scale_table[:].indirect(k1_sb[:]))
-        planes = sb.tile([P, H + S], U8, align_bytes=64)
-        nc.vector.tensor_copy(
-            out=dealt_view(planes[:, 0:H], 16),
-            in_=plain_view(d_scale_picked[:], 16),
-        )
         x_scale_picked = sb.tile([P, S], U8, tag="x_scale_picked", align_bytes=64)
         nc.vector.tensor_copy(out=x_scale_picked[:], in_=x_scale_table[:].indirect(offs_sb[:]))
+        planes = sb.tile([P, H + S], U8, align_bytes=64)
+        deal(nc.vector.tensor_copy, planes[:, 0:H], d_scale_picked[:], 1)
         nc.vector.tensor_copy(out=planes[:, H : H + S].bitcast(I32), in_=x_scale_picked[:].bitcast(I32))
-        for s in range(1, 4):
-            nc.scalar.dma_start(out=planes[s:P:32, :].bitcast(I32), in_=planes[8 * s : P : 32, :].bitcast(I32))
+        rows_to_plane(nc.scalar, planes)
 
         w1_dealt = sb.tile([P, 2 * N], U8, tag="x_scale_picked", align_bytes=64)
-        nc.scalar.copy(
-            out=dealt_view(w1_dealt[:].bitcast(U16), 8),
-            in_=plain_view(w1_raw[:].bitcast(U16), 8),
-        )
+        deal(nc.scalar.copy, w1_dealt[:].bitcast(U16), w1_raw[:].bitcast(U16), 2)
 
         d_picked = sb.tile([P, H], U32, tag="x_scale_table", align_bytes=64)
         nc.vector.tensor_copy(out=d_picked[:], in_=d_word_table[:].bitcast(U32).indirect(k1_sb[:]))
         d_dealt = sb.tile([P, H], U32, align_bytes=64)
-        nc.vector.tensor_copy(
-            out=dealt_view(d_dealt[:], 4), in_=plain_view(d_picked[:], 4)
-        )
+        deal(nc.vector.tensor_copy, d_dealt[:], d_picked[:], 4)
         x_picked = []
-        for c in range(2):
-            tile = sb.tile([P, HALF_S], U32, name="x_picked%d" % c, tag=("d_word_table", "x_scale_table")[c], align_bytes=64)
-            cols = slice(c * HALF_S // PER_COL, (c + 1) * HALF_S // PER_COL)
-            nc.vector.tensor_copy(out=tile[:], in_=x_word_table[:].bitcast(U32).indirect(offs_sb[:, cols]))
+        for c, buffer in enumerate(("d_word_table", "x_scale_table")):
+            tile = sb.tile([P, HALF_S], U32, name="x_picked%d" % c, tag=buffer, align_bytes=64)
+            nc.vector.tensor_copy(out=tile[:], in_=x_word_table[:].bitcast(U32).indirect(entries(offs_sb, c, HALF_S)))
             x_picked.append(tile)
         w1_scale_dealt = sb.tile([P, N], U8, tag="x_word_table", align_bytes=64)
-        nc.vector.tensor_copy(
-            out=dealt_view(w1_scale_dealt[:], 16),
-            in_=plain_view(w1_scale_raw[:], 16),
-        )
-        for s in range(1, 4):
-            nc.sync.dma_start(
-                out=w1_scale_dealt[s:P:32, :].bitcast(I32), in_=w1_scale_dealt[8 * s : P : 32, :].bitcast(I32)
-            )
+        deal(nc.vector.tensor_copy, w1_scale_dealt[:], w1_scale_raw[:], 1)
+        rows_to_plane(nc.sync, w1_scale_dealt)
 
-        squares = [sb.tile([P, S], F32, name="squares%d" % t) for t in range(PACK)]
-        for t, c in ((0, 0), (1, 0), (0, 1), (1, 1), (2, 0), (2, 1), (3, 0), (3, 1)):
+        squares = [sb.tile([P, S], F32, name="squares%d" % t, tag="squares%d" % t) for t in range(PACK)]
+        first_couple = [(t, c) for c in range(2) for t in (0, 1)]
+        second_couple = [(t, c) for t in (2, 3) for c in range(2)]
+        for t, c in first_couple + second_couple:
             bank = ps.tile([P, HALF_S], F32, name="h_bank", tag="bank%d" % (2 * t + c))
             nc.tensor.matmul_mx(
                 out=bank[:],
@@ -128,45 +132,57 @@ def tile_picked_hpqhprmstrack_none_po_kernel(
                 out=squares[t][:, c * HALF_S : (c + 1) * HALF_S], in_=bank[:], func=ACT.Square, scale=0.0625
             )
 
-        lined = [sb.tile([P, PACK, HALF_S], F32, name="lined%d" % c) for c in range(2)]
-
-        def line_up(t, c, on_scalar):
-            window = squares[t][:].indirect(n1_sb[:, c * HALF_S // PER_COL : (c + 1) * HALF_S // PER_COL])
-            if on_scalar:
-                nc.scalar.activation(out=lined[c][:, t, :], in_=window, func=ACT.Copy)
-            else:
-                nc.vector.tensor_copy(out=lined[c][:, t, :], in_=window)
-
+        lined = {(c, u): sb.tile([P, 2, HALF_S], F32, name="lined%d%d" % (c, u)) for c, u in ((0, 0), (0, 1), (1, 0))}
         for t in range(PACK):
-            line_up(t, 0, False)
-        for t in range(PACK):
-            line_up(t, 1, t != 2)
+            window = squares[t][:].indirect(entries(n1_sb, 0, HALF_S))
+            nc.vector.tensor_copy(out=lined[0, t // 2][:, t % 2, :], in_=window)
+        for t in (0, 1):
+            window = squares[t][:].indirect(entries(n1_sb, 1, HALF_S))
+            nc.scalar.activation(out=lined[1, 0][:, t, :], in_=window, func=ACT.Copy)
+        lined[1, 1] = sb.tile([P, 2, HALF_S], F32, name="lined11", tag="squares0")
+        for t in (2, 3):
+            window = squares[t][:].indirect(entries(n1_sb, 1, HALF_S))
+            nc.vector.tensor_copy(out=lined[1, 1][:, t - 2, :], in_=window)
 
-        h2_rows = [sb.tile([P, V], F32, name="h2_rows%d" % t) for t in range(PACK)]
-        h2_banks, z_mx = [], []
-        sums, roots = [], []
+        sums = []
         for c in range(2):
             pair_sums = sb.tile([P, PACK, HALF_V], F32, name="pair_sums%d" % c)
-            pairs = lined[c][:].rearrange("p t (v e) -> p (t v) e", e=2)
-            nc.vector.tensor_tensor(
-                out=pair_sums[:].rearrange("p t v -> p (t v)"), in0=pairs[:, :, 0], in1=pairs[:, :, 1], op=ALU.add
-            )
+            for u in range(2):
+                neighbours = lined[c, u][:].rearrange("p t (v e) -> p (t v) e", e=2)
+                engine = nc.vector if (c, u) == (1, 1) else nc.gpsimd
+                engine.tensor_tensor(
+                    out=couple(pair_sums, u).rearrange("p t v -> p (t v)"),
+                    in0=neighbours[:, :, 0],
+                    in1=neighbours[:, :, 1],
+                    op=ALU.add,
+                )
             sums.append(pair_sums)
+
+        parts = ([slice(0, HALF_V)], [slice(0, HALF_V // 2), slice(HALF_V // 2, HALF_V)])
+        roots = []
         for c in range(2):
             root = sb.tile([P, HALF_V, PACK], F32, name="root%d" % c)
-            nc.scalar.activation(out=root[:], in_=sums[c][:].rearrange("p t v -> p v t"), func=ACT.Sqrt, bias=0.1)
+            for cols in parts[c]:
+                nc.scalar.activation(
+                    out=root[:, cols, :], in_=sums[c][:, :, cols].rearrange("p t v -> p v t"), func=ACT.Sqrt, bias=0.1
+                )
             roots.append(root)
+
+        z_mx = []
         for c in range(2):
             z = sb.tile([P, HALF_V, PACK], BF16, name="z%d" % c, align_bytes=64)
-            nc.vector.tensor_tensor(
-                out=z[:], in0=roots[c][:], in1=gain[:].unsqueeze(1).to_broadcast([P, HALF_V, PACK]), op=ALU.mult
-            )
+            for cols in parts[c]:
+                spread = gain[:].unsqueeze(1).to_broadcast([P, cols.stop - cols.start, PACK])
+                nc.vector.tensor_tensor(out=z[:, cols, :], in0=roots[c][:, cols, :], in1=spread, op=ALU.mult)
             z_codes = sb.tile([P, HALF_V], U32, name="z_codes%d" % c, align_bytes=64)
             z_scales = sb.tile([P, HALF_V], U8, name="z_scales%d" % c, align_bytes=64)
             nc.vector.quantize_mx(
                 out=z_codes[:].bitcast(FP8X4), scales=z_scales[:], in_=z[:].rearrange("p v t -> p (v t)")
             )
             z_mx.append((z_codes, z_scales))
+
+        h2_rows = [sb.tile([P, V], F32, name="h2_rows%d" % t) for t in range(PACK)]
+        h2_banks = []
         for u in range(2):
             bank = ps.tile([P, 2, V], F32, name="h2_bank", tag="bank%d" % u)
             for c in range(2):
@@ -185,76 +201,70 @@ def tile_picked_hpqhprmstrack_none_po_kernel(
                 nc.vector.tensor_copy(out=h2_rows[2 * u + e][:], in_=bank[:, e, :])
             h2_banks.append(bank)
 
-        def half_of(lst, c):
-            return lst[:, c * HALF_V // PER_COL : (c + 1) * HALF_V // PER_COL]
-
         gates = [sb.tile([P, PACK, HALF_V], F32, name="gates%d" % c) for c in range(2)]
-        other = [sb.tile([P, PACK, HALF_V], F32, name="other%d" % c) for c in range(2)]
-        mid = [sb.tile([P, PACK, HALF_V], F32, name="mid%d" % c) for c in range(2)]
+        gated_far = sb.tile([P, PACK, HALF_V], F32)
+        far = sb.tile([P, PACK, HALF_V], F32)
+        less_own = sb.tile([P, PACK, HALF_V], F32)
+        gated_diff = sb.tile([P, PACK, HALF_V], F32)
         result = [sb.tile([P, PACK, HALF_V], F32, name="result%d" % c) for c in range(2)]
         for t in range(PACK):
-            nc.scalar.activation(out=gates[0][:, t, :], in_=h2_rows[t][:].indirect(half_of(n2_sb, 0)), func=ACT.Sigmoid)
+            window = h2_rows[t][:].indirect(entries(n2_sb, 0, HALF_V))
+            nc.scalar.activation(out=gates[0][:, t, :], in_=window, func=ACT.Sigmoid)
         for u in range(2):
             for t in (2 * u, 2 * u + 1):
-                nc.scalar.activation(out=other[1][:, t, :], in_=h2_rows[t][:].indirect(half_of(n3_sb, 1)), func=ACT.Copy)
+                window = h2_rows[t][:].indirect(entries(n3_sb, 1, HALF_V))
+                nc.scalar.activation(out=far[:, t, :], in_=window, func=ACT.Copy)
             for t in (2 * u, 2 * u + 1):
-                nc.scalar.activation(
-                    out=gates[1][:, t, :], in_=h2_rows[t][:].indirect(half_of(n2_sb, 1)), func=ACT.Sigmoid
-                )
-
-        def pair(tile, u):
-            return tile[:, 2 * u : 2 * u + 2, :]
-
-        def flat(tile):
-            return tile[:].rearrange("p t v -> p (t v)")
+                window = h2_rows[t][:].indirect(entries(n2_sb, 1, HALF_V))
+                nc.scalar.activation(out=gates[1][:, t, :], in_=window, func=ACT.Sigmoid)
 
         for u in range(2):
             for t in (2 * u, 2 * u + 1):
-                nc.vector.tensor_tensor(
-                    out=other[0][:, t, :],
-                    in0=h2_rows[t][:].indirect(half_of(n3_sb, 0)),
-                    in1=gates[0][:, t, :],
-                    op=ALU.mult,
-                )
+                window = h2_rows[t][:].indirect(entries(n3_sb, 0, HALF_V))
+                nc.vector.tensor_tensor(out=gated_far[:, t, :], in0=window, in1=gates[0][:, t, :], op=ALU.mult)
             nc.vector.scalar_tensor_tensor(
-                out=pair(mid[0], u),
-                in0=pair(gates[0], u),
+                out=couple(less_own, u),
+                in0=couple(gates[0], u),
                 scalar=1.0,
                 in1=h2_banks[u][:, :, 0:HALF_V],
                 op0=ALU.subtract,
                 op1=ALU.mult,
             )
-        nc.vector.tensor_tensor(out=flat(result[0]), in0=flat(other[0]), in1=flat(mid[0]), op=ALU.subtract)
+        nc.vector.tensor_tensor(out=flat(result[0]), in0=flat(gated_far), in1=flat(less_own), op=ALU.subtract)
+
         diff = sb.tile([P, PACK, HALF_V], F32)
         for u in range(2):
-            nc.vector.tensor_tensor(out=pair(diff, u), in0=pair(other[1], u), in1=h2_banks[u][:, :, HALF_V:V], op=ALU.subtract)
-            nc.vector.tensor_tensor(out=pair(mid[1], u), in0=pair(diff, u), in1=pair(gates[1], u), op=ALU.mult)
-            nc.vector.tensor_tensor(out=pair(result[1], u), in0=pair(mid[1], u), in1=h2_banks[u][:, :, HALF_V:V], op=ALU.add)
+            own = h2_banks[u][:, :, HALF_V:V]
+            nc.vector.tensor_tensor(out=couple(diff, u), in0=couple(far, u), in1=own, op=ALU.subtract)
+            nc.vector.tensor_tensor(out=couple(gated_diff, u), in0=couple(diff, u), in1=couple(gates[1], u), op=ALU.mult)
+            nc.vector.tensor_tensor(out=couple(result[1], u), in0=couple(gated_diff, u), in1=own, op=ALU.add)
 
         out_rows = out_0.rearrange("(p t) v -> p t v", t=PACK)
         out_words = out_1[0].rearrange("p v t -> p (v t)").bitcast(I32)
         out_scales = sb.tile([P, V], U8, align_bytes=64)
-        for c in range(2):
+
+        def store_planes(c, copy):
             cols = slice(c * HALF_V, (c + 1) * HALF_V)
-            if c == 0:
-                nc.sync.dma_start(out=out_rows[:, :, cols], in_=result[c][:])
-            else:
-                for u in range(2):
-                    nc.sync.dma_start(out=out_rows[:, 2 * u : 2 * u + 2, cols], in_=pair(result[c], u))
             out_bf = sb.tile([P, HALF_V, PACK], BF16, name="out_bf%d" % c, align_bytes=64)
-            woven = out_bf[:].rearrange("p (a i) t -> p a t i", i=4)
-            runs = result[c][:].rearrange("p t (a i) -> p a t i", i=4)
-            if c == 0:
-                nc.scalar.copy(out=woven, in_=runs)
-            else:
-                nc.vector.tensor_copy(out=woven, in_=runs)
+            copy(
+                out=out_bf[:].rearrange("p (a i) t -> p a t i", i=4),
+                in_=result[c][:].rearrange("p t (a i) -> p a t i", i=4),
+            )
             out_codes = sb.tile([P, HALF_V], I32, name="out_codes%d" % c, align_bytes=64)
             nc.vector.quantize_mx(
                 out=out_codes[:].bitcast(FP8X4), scales=out_scales[:, cols], in_=out_bf[:].rearrange("p v t -> p (v t)")
             )
             nc.sync.dma_start(out=out_words[:, cols], in_=out_codes[:])
-        for q in range(4):
+
+        nc.sync.dma_start(out=out_rows[:, :, 0:HALF_V], in_=result[0][:])
+        store_planes(0, nc.scalar.copy)
+        for u in range(2):
+            nc.sync.dma_start(out=out_rows[:, 2 * u : 2 * u + 2, HALF_V:V], in_=couple(result[1], u))
+        store_planes(1, nc.vector.tensor_copy)
+
+        for q in range(P // QUADRANT):
             queue = nc.scalar if q % 2 == 0 else nc.sync
             queue.dma_start(
-                out=out_2[0, 4 * q : 4 * q + 4, :].bitcast(I32), in_=out_scales[32 * q : 32 * q + 4, :].bitcast(I32)
+                out=out_2[0, PACK * q : PACK * (q + 1), :].bitcast(I32),
+                in_=out_scales[QUADRANT * q : QUADRANT * q + PACK, :].bitcast(I32),
             )

from contextlib import ExitStack

import concourse.mybir as mybir

K, T, S, V, N, H = 512, 2048, 512, 256, 512, 512
FLOPS = 2 * K * H * S + 2 * H * N * V

F32 = mybir.dt.float32
BF16 = mybir.dt.bfloat16
I32 = mybir.dt.int32
U32 = mybir.dt.uint32
U16 = mybir.dt.uint16
U8 = mybir.dt.uint8
FP8X4 = mybir.dt.float8_e4m3fn_x4
FP4X4 = mybir.dt.float4_e2m1fn_x4
ACT = mybir.ActivationFunctionType
ALU = mybir.AluOpType

P = 128
PACK = 4
QUADRANT = 32
BLOCK_PARTS = 8
SCALE_ROWS = P // BLOCK_PARTS
PER_COL = 16
LINE = 16
HALF_S = S // 2
HALF_V = V // 2


def tile_picked_hpqhprmstrack_none_po_kernel(
    tc, x_words, x_scales, d_words, d_scales, gn, w1_words, w1_scales, offs, k1, n1, n2, n3, out_0, out_1, out_2
):
    nc = tc.nc
    with ExitStack() as ctx:
        sb = ctx.enter_context(tc.tile_pool(name="sb", bufs=1))
        ps = ctx.enter_context(tc.psum_pool(name="ps", bufs=1))

        def load_list(src, name):
            tile = sb.tile(list(src.shape), U16, name=name)
            nc.sync.dma_start(out=tile[:], in_=src)
            return tile

        def load_scale_rows(src, name):
            width = src.shape[2]
            tile = sb.tile([P, width], U8, name=name, tag=name, align_bytes=64)
            rows = src[0].bitcast(I32).unsqueeze(1).to_broadcast([SCALE_ROWS, BLOCK_PARTS, width // 4])
            nc.sync.dma_start(out=tile[:].bitcast(I32), in_=rows)
            return tile

        def load_word_table(src, name):
            tile = sb.tile([P, T], I32, name=name, tag=name, align_bytes=64)
            nc.sync.dma_start(out=tile[:], in_=src[0].rearrange("p n t -> p (n t)").bitcast(I32))
            return tile

        def deal(copy, dst, src, elem_bytes):
            run = LINE // elem_bytes
            copy(
                out=dst.rearrange("p (t a i) -> p a t i", t=PACK, i=run),
                in_=src.rearrange("p (a i t) -> p a t i", t=PACK, i=run),
            )

        def rows_to_plane(queue, tile):
            for s in range(1, PACK):
                queue.dma_start(
                    out=tile[s:P:QUADRANT, :].bitcast(I32), in_=tile[BLOCK_PARTS * s : P : QUADRANT, :].bitcast(I32)
                )

        def entries(list_tile, c, count):
            return list_tile[:, c * count // PER_COL : (c + 1) * count // PER_COL]

        def couple(tile, u):
            return tile[:, 2 * u : 2 * u + 2, :]

        def flat(tile):
            return tile[:].rearrange("p t v -> p (t v)")

        d_scale_table = load_scale_rows(d_scales, "d_scale_table")
        k1_sb = load_list(k1, "k1_sb")
        x_scale_table = load_scale_rows(x_scales, "x_scale_table")
        offs_sb = load_list(offs, "offs_sb")
        d_word_table = load_word_table(d_words, "d_word_table")
        n1_sb = load_list(n1, "n1_sb")
        n2_sb = load_list(n2, "n2_sb")
        x_word_table = load_word_table(x_words, "x_word_table")
        n3_sb = load_list(n3, "n3_sb")
        w1_raw = sb.tile([P, 2 * N], U8, align_bytes=64)
        nc.sync.dma_start(out=w1_raw[:].bitcast(I32), in_=w1_words[0].bitcast(I32))
        gain = sb.tile([P, PACK], F32)
        nc.sync.dma_start(out=gain[:], in_=gn.rearrange("(p t) o -> p (t o)", t=PACK))
        w1_scale_raw = load_scale_rows(w1_scales, "w1_scale_raw")

        d_scale_picked = sb.tile([P, H], U8, align_bytes=64)
        nc.vector.tensor_copy(out=d_scale_picked[:], in_=d_scale_table[:].indirect(k1_sb[:]))
        x_scale_picked = sb.tile([P, S], U8, tag="x_scale_picked", align_bytes=64)
        nc.vector.tensor_copy(out=x_scale_picked[:], in_=x_scale_table[:].indirect(offs_sb[:]))
        planes = sb.tile([P, H + S], U8, align_bytes=64)
        deal(nc.vector.tensor_copy, planes[:, 0:H], d_scale_picked[:], 1)
        nc.vector.tensor_copy(out=planes[:, H : H + S].bitcast(I32), in_=x_scale_picked[:].bitcast(I32))
        rows_to_plane(nc.scalar, planes)

        w1_dealt = sb.tile([P, 2 * N], U8, tag="x_scale_picked", align_bytes=64)
        deal(nc.scalar.copy, w1_dealt[:].bitcast(U16), w1_raw[:].bitcast(U16), 2)

        d_picked = sb.tile([P, H], U32, tag="x_scale_table", align_bytes=64)
        nc.vector.tensor_copy(out=d_picked[:], in_=d_word_table[:].bitcast(U32).indirect(k1_sb[:]))
        d_dealt = sb.tile([P, H], U32, align_bytes=64)
        deal(nc.vector.tensor_copy, d_dealt[:], d_picked[:], 4)
        x_picked = []
        for c, buffer in enumerate(("d_word_table", "x_scale_table")):
            tile = sb.tile([P, HALF_S], U32, name="x_picked%d" % c, tag=buffer, align_bytes=64)
            nc.vector.tensor_copy(out=tile[:], in_=x_word_table[:].bitcast(U32).indirect(entries(offs_sb, c, HALF_S)))
            x_picked.append(tile)
        w1_scale_dealt = sb.tile([P, N], U8, tag="x_word_table", align_bytes=64)
        deal(nc.vector.tensor_copy, w1_scale_dealt[:], w1_scale_raw[:], 1)
        rows_to_plane(nc.sync, w1_scale_dealt)

        squares = [sb.tile([P, S], F32, name="squares%d" % t, tag="squares%d" % t) for t in range(PACK)]
        first_couple = [(t, c) for c in range(2) for t in (0, 1)]
        second_couple = [(t, c) for t in (2, 3) for c in range(2)]
        for t, c in first_couple + second_couple:
            bank = ps.tile([P, HALF_S], F32, name="h_bank", tag="bank%d" % (2 * t + c))
            nc.tensor.matmul_mx(
                out=bank[:],
                lhsT=d_dealt[:, t * P : (t + 1) * P].bitcast(FP8X4),
                lhsT_scale=planes[:, t * P : (t + 1) * P],
                rhs=x_picked[c][:].bitcast(FP8X4),
                rhs_scale=planes[:, H + c * HALF_S : H + (c + 1) * HALF_S],
                start=True,
                stop=True,
            )
            nc.scalar.activation(
                out=squares[t][:, c * HALF_S : (c + 1) * HALF_S], in_=bank[:], func=ACT.Square, scale=0.0625
            )

        lined = {(c, u): sb.tile([P, 2, HALF_S], F32, name="lined%d%d" % (c, u)) for c, u in ((0, 0), (0, 1), (1, 0))}
        for t in range(PACK):
            window = squares[t][:].indirect(entries(n1_sb, 0, HALF_S))
            nc.vector.tensor_copy(out=lined[0, t // 2][:, t % 2, :], in_=window)
        for t in (0, 1):
            window = squares[t][:].indirect(entries(n1_sb, 1, HALF_S))
            nc.scalar.activation(out=lined[1, 0][:, t, :], in_=window, func=ACT.Copy)
        lined[1, 1] = sb.tile([P, 2, HALF_S], F32, name="lined11", tag="squares0")
        for t in (2, 3):
            window = squares[t][:].indirect(entries(n1_sb, 1, HALF_S))
            nc.vector.tensor_copy(out=lined[1, 1][:, t - 2, :], in_=window)

        sums = []
        for c in range(2):
            pair_sums = sb.tile([P, PACK, HALF_V], F32, name="pair_sums%d" % c)
            for u in range(2):
                neighbours = lined[c, u][:].rearrange("p t (v e) -> p (t v) e", e=2)
                engine = nc.vector if (c, u) == (1, 1) else nc.gpsimd
                engine.tensor_tensor(
                    out=couple(pair_sums, u).rearrange("p t v -> p (t v)"),
                    in0=neighbours[:, :, 0],
                    in1=neighbours[:, :, 1],
                    op=ALU.add,
                )
            sums.append(pair_sums)

        parts = ([slice(0, HALF_V)], [slice(0, HALF_V // 2), slice(HALF_V // 2, HALF_V)])
        roots = []
        for c in range(2):
            root = sb.tile([P, HALF_V, PACK], F32, name="root%d" % c)
            for cols in parts[c]:
                nc.scalar.activation(
                    out=root[:, cols, :], in_=sums[c][:, :, cols].rearrange("p t v -> p v t"), func=ACT.Sqrt, bias=0.1
                )
            roots.append(root)

        z_mx = []
        for c in range(2):
            z = sb.tile([P, HALF_V, PACK], BF16, name="z%d" % c, align_bytes=64)
            for cols in parts[c]:
                spread = gain[:].unsqueeze(1).to_broadcast([P, cols.stop - cols.start, PACK])
                nc.vector.tensor_tensor(out=z[:, cols, :], in0=roots[c][:, cols, :], in1=spread, op=ALU.mult)
            z_codes = sb.tile([P, HALF_V], U32, name="z_codes%d" % c, align_bytes=64)
            z_scales = sb.tile([P, HALF_V], U8, name="z_scales%d" % c, align_bytes=64)
            nc.vector.quantize_mx(
                out=z_codes[:].bitcast(FP8X4), scales=z_scales[:], in_=z[:].rearrange("p v t -> p (v t)")
            )
            z_mx.append((z_codes, z_scales))

        h2_rows = [sb.tile([P, V], F32, name="h2_rows%d" % t) for t in range(PACK)]
        h2_banks = []
        for u in range(2):
            bank = ps.tile([P, 2, V], F32, name="h2_bank", tag="bank%d" % u)
            for c in range(2):
                for e in range(2):
                    t = 2 * u + e
                    nc.tensor.matmul_mx(
                        out=bank[:, e, c * HALF_V : (c + 1) * HALF_V],
                        lhsT=w1_dealt[:, 2 * t * P : 2 * (t + 1) * P].bitcast(FP4X4),
                        lhsT_scale=w1_scale_dealt[:, t * P : (t + 1) * P],
                        rhs=z_mx[c][0][:].bitcast(FP8X4),
                        rhs_scale=z_mx[c][1][:],
                        start=True,
                        stop=True,
                    )
            for e in range(2):
                nc.vector.tensor_copy(out=h2_rows[2 * u + e][:], in_=bank[:, e, :])
            h2_banks.append(bank)

        gates = [sb.tile([P, PACK, HALF_V], F32, name="gates%d" % c) for c in range(2)]
        gated_far = sb.tile([P, PACK, HALF_V], F32)
        far = sb.tile([P, PACK, HALF_V], F32)
        less_own = sb.tile([P, PACK, HALF_V], F32)
        gated_diff = sb.tile([P, PACK, HALF_V], F32)
        result = [sb.tile([P, PACK, HALF_V], F32, name="result%d" % c) for c in range(2)]
        for t in range(PACK):
            window = h2_rows[t][:].indirect(entries(n2_sb, 0, HALF_V))
            nc.scalar.activation(out=gates[0][:, t, :], in_=window, func=ACT.Sigmoid)
        for u in range(2):
            for t in (2 * u, 2 * u + 1):
                window = h2_rows[t][:].indirect(entries(n3_sb, 1, HALF_V))
                nc.scalar.activation(out=far[:, t, :], in_=window, func=ACT.Copy)
            for t in (2 * u, 2 * u + 1):
                window = h2_rows[t][:].indirect(entries(n2_sb, 1, HALF_V))
                nc.scalar.activation(out=gates[1][:, t, :], in_=window, func=ACT.Sigmoid)

        for u in range(2):
            for t in (2 * u, 2 * u + 1):
                window = h2_rows[t][:].indirect(entries(n3_sb, 0, HALF_V))
                nc.vector.tensor_tensor(out=gated_far[:, t, :], in0=window, in1=gates[0][:, t, :], op=ALU.mult)
            nc.vector.scalar_tensor_tensor(
                out=couple(less_own, u),
                in0=couple(gates[0], u),
                scalar=1.0,
                in1=h2_banks[u][:, :, 0:HALF_V],
                op0=ALU.subtract,
                op1=ALU.mult,
            )
        nc.vector.tensor_tensor(out=flat(result[0]), in0=flat(gated_far), in1=flat(less_own), op=ALU.subtract)

        diff = sb.tile([P, PACK, HALF_V], F32)
        for u in range(2):
            own = h2_banks[u][:, :, HALF_V:V]
            nc.vector.tensor_tensor(out=couple(diff, u), in0=couple(far, u), in1=own, op=ALU.subtract)
            nc.vector.tensor_tensor(out=couple(gated_diff, u), in0=couple(diff, u), in1=couple(gates[1], u), op=ALU.mult)
            nc.vector.tensor_tensor(out=couple(result[1], u), in0=couple(gated_diff, u), in1=own, op=ALU.add)

        out_rows = out_0.rearrange("(p t) v -> p t v", t=PACK)
        out_words = out_1[0].rearrange("p v t -> p (v t)").bitcast(I32)
        out_scales = sb.tile([P, V], U8, align_bytes=64)

        def store_planes(c, copy):
            cols = slice(c * HALF_V, (c + 1) * HALF_V)
            out_bf = sb.tile([P, HALF_V, PACK], BF16, name="out_bf%d" % c, align_bytes=64)
            copy(
                out=out_bf[:].rearrange("p (a i) t -> p a t i", i=4),
                in_=result[c][:].rearrange("p t (a i) -> p a t i", i=4),
            )
            out_codes = sb.tile([P, HALF_V], I32, name="out_codes%d" % c, align_bytes=64)
            nc.vector.quantize_mx(
                out=out_codes[:].bitcast(FP8X4), scales=out_scales[:, cols], in_=out_bf[:].rearrange("p v t -> p (v t)")
            )
            nc.sync.dma_start(out=out_words[:, cols], in_=out_codes[:])

        nc.sync.dma_start(out=out_rows[:, :, 0:HALF_V], in_=result[0][:])
        store_planes(0, nc.scalar.copy)
        for u in range(2):
            nc.sync.dma_start(out=out_rows[:, 2 * u : 2 * u + 2, HALF_V:V], in_=couple(result[1], u))
        store_planes(1, nc.vector.tensor_copy)

        for q in range(P // QUADRANT):
            queue = nc.scalar if q % 2 == 0 else nc.sync
            queue.dma_start(
                out=out_2[0, PACK * q : PACK * (q + 1), :].bitcast(I32),
                in_=out_scales[QUADRANT * q : QUADRANT * q + PACK, :].bitcast(I32),
            )
